import numpy as np
import ml_dtypes

BF16 = ml_dtypes.bfloat16


def bf(x):
    return np.asarray(x, np.float32).astype(BF16)


def f32(x):
    return np.asarray(x, np.float32)


def f64(x):
    return np.asarray(x).astype(np.float64)


def striped(idx):
    return np.concatenate([l.reshape(-1, 16).T for l in idx])


def rows(idx, k):
    return np.tile(np.repeat(idx, 16, axis=0), (k // (16 * 8), 1))


def look(tab, idx):
    return np.take_along_axis(f64(tab), rows(idx, len(tab)), axis=1)


K, S, V, N, M = 256, 2048, 2048, 2048, 256


def silu(v):
    return v / (1.0 + np.exp(-v))


def setup_inputs():
    return {"tab": f32(np.random.standard_normal((2, K, S))), "y": f32(np.random.standard_normal((K, V))), "w": bf(np.random.standard_normal((K, M)) / np.sqrt(K)), "b": f32(0.5 * np.random.standard_normal((M, 1))), "offs": striped(np.stack([np.random.permutation(S)[:N] for _ in range(8)]))}


def reference(tab, y, w, b, offs):
    idx = np.stack([g.T.reshape(-1) for g in np.split(offs, 8)])
    x = (np.maximum(look(tab[0], idx), f64(y))) * (silu(look(tab[1], idx)))
    return np.maximum(f64(w).T @ x + f64(b), 0.0)

@@ -1,0 +1,72 @@
+import concourse.mybir as mybir
+
+F32, BF16, U16 = mybir.dt.float32, mybir.dt.bfloat16, mybir.dt.uint16
+MAX, MULT = mybir.AluOpType.max, mybir.AluOpType.mult
+SILU, RELU = mybir.ActivationFunctionType.Silu, mybir.ActivationFunctionType.Relu
+
+P = 128
+PIECE = 512
+FLOPS = 2 * 256 * 256 * 2048
+
+
+def tile_lookup_vg_maxsilu_relu_kernel(tc, tab, y, w, b, offs, out):
+    nc = tc.nc
+    rows, places = tab.shape[1], tab.shape[2]
+    n = y.shape[1]
+    width = w.shape[1]
+    row_blocks, out_blocks, pieces = rows // P, width // P, n // PIECE
+    piece_offsets = PIECE // 16
+
+    with (
+        tc.tile_pool(name="held", bufs=1) as held,
+        tc.tile_pool(name="work", bufs=3) as work,
+        tc.psum_pool(name="psum", bufs=1) as psum,
+    ):
+        offsets = held.tile([P, n // 16], U16, name="offsets")
+        nc.sync.dma_start(offsets[:], offs)
+
+        values, gates, streams = [], [], []
+        for r in range(row_blocks):
+            block = slice(r * P, (r + 1) * P)
+            gate = held.tile([P, places], F32, name=f"gate{r}")
+            nc.sync.dma_start(gate[:], tab[1, block, :])
+            value = held.tile([P, places], F32, name=f"value{r}")
+            nc.sync.dma_start(value[:], tab[0, block, :])
+            stream = held.tile([P, n], F32, name=f"stream{r}")
+            nc.sync.dma_start(stream[:], y[block, :])
+            gates.append(gate)
+            values.append(value)
+            streams.append(stream)
+
+        weights = held.tile([P, row_blocks, width], BF16, name="weights")
+        nc.scalar.dma_start(weights[:], w.rearrange("(r p) m -> p r m", p=P))
+        bias = held.tile([P, out_blocks], F32, name="bias")
+        with nc.allow_non_contiguous_dma(reason="256 single values, one to a partition and block"):
+            nc.scalar.dma_start(bias[:], b.rearrange("(m p) o -> p (m o)", p=P))
+
+        sums = [[psum.tile([P, PIECE], F32, name=f"sum{m}_{c}") for c in range(pieces)] for m in range(out_blocks)]
+
+        for r in range(row_blocks):
+            for c in range(pieces):
+                columns = slice(c * PIECE, (c + 1) * PIECE)
+                listed = offsets[:, c * piece_offsets : (c + 1) * piece_offsets]
+                silu = work.tile([P, PIECE], F32, name="silu")
+                nc.scalar.activation(silu[:], gates[r][:].indirect(listed), SILU)
+                top = work.tile([P, PIECE], F32, name="top")
+                nc.vector.tensor_tensor(top[:], values[r][:].indirect(listed), streams[r][:, columns], MAX)
+                x = work.tile([P, PIECE], BF16, name="x")
+                nc.vector.tensor_tensor(x[:], top[:], silu[:], MULT)
+                for m in range(out_blocks):
+                    nc.tensor.matmul(
+                        sums[m][c][:],
+                        weights[:, r, m * P : (m + 1) * P],
+                        x[:],
+                        start=r == 0,
+                        stop=r == row_blocks - 1,
+                    )
+
+        for c in range(pieces):
+            for m in range(out_blocks):
+                result = work.tile([P, PIECE], F32, name="result")
+                nc.scalar.activation(result[:], sums[m][c][:], RELU, bias=bias[:, m : m + 1])
+                nc.sync.dma_start(out[m * P : (m + 1) * P, c * PIECE : (c + 1) * PIECE], result[:])

@@ -1,7 +1,7 @@
 import concourse.mybir as mybir
 
 F32, BF16, U16 = mybir.dt.float32, mybir.dt.bfloat16, mybir.dt.uint16
-MAX, MULT = mybir.AluOpType.max, mybir.AluOpType.mult
+ADD, MAX, MULT = mybir.AluOpType.add, mybir.AluOpType.max, mybir.AluOpType.mult
 SILU, RELU = mybir.ActivationFunctionType.Silu, mybir.ActivationFunctionType.Relu
 
 P = 128
@@ -19,30 +19,32 @@ def tile_lookup_vg_maxsilu_relu_kernel(tc, tab, y, w, b, offs, out):
 
     with (
         tc.tile_pool(name="held", bufs=1) as held,
-        tc.tile_pool(name="work", bufs=3) as work,
+        tc.tile_pool(name="work", bufs=row_blocks * pieces) as work,
         tc.psum_pool(name="psum", bufs=1) as psum,
     ):
         offsets = held.tile([P, n // 16], U16, name="offsets")
         nc.sync.dma_start(offsets[:], offs)
 
         values, gates, streams = [], [], []
+        half = n // 2
         for r in range(row_blocks):
             block = slice(r * P, (r + 1) * P)
-            gate = held.tile([P, places], F32, name=f"gate{r}")
-            nc.sync.dma_start(gate[:], tab[1, block, :])
             value = held.tile([P, places], F32, name=f"value{r}")
-            nc.sync.dma_start(value[:], tab[0, block, :])
+            gate = held.tile([P, places], F32, name=f"gate{r}")
             stream = held.tile([P, n], F32, name=f"stream{r}")
-            nc.sync.dma_start(stream[:], y[block, :])
-            gates.append(gate)
+            nc.sync.dma_start(value[:], tab[0, block, :])
+            nc.sync.dma_start(stream[:, :half], y[block, :half])
+            nc.sync.dma_start(gate[:], tab[1, block, :])
+            nc.sync.dma_start(stream[:, half:], y[block, half:])
             values.append(value)
+            gates.append(gate)
             streams.append(stream)
-
-        weights = held.tile([P, row_blocks, width], BF16, name="weights")
-        nc.scalar.dma_start(weights[:], w.rearrange("(r p) m -> p r m", p=P))
-        bias = held.tile([P, out_blocks], F32, name="bias")
-        with nc.allow_non_contiguous_dma(reason="256 single values, one to a partition and block"):
-            nc.scalar.dma_start(bias[:], b.rearrange("(m p) o -> p (m o)", p=P))
+            if r == 0:
+                weights = held.tile([P, row_blocks, width], BF16, name="weights")
+                nc.sync.dma_start(weights[:], w.rearrange("(k p) m -> p k m", p=P))
+                bias = held.tile([P, out_blocks], F32, name="bias")
+                with nc.allow_non_contiguous_dma(reason="256 single values, one to a partition and block"):
+                    nc.sync.dma_start(bias[:], b.rearrange("(m p) o -> p (m o)", p=P))
 
         sums = [[psum.tile([P, PIECE], F32, name=f"sum{m}_{c}") for c in range(pieces)] for m in range(out_blocks)]
 
@@ -65,8 +67,11 @@ def tile_lookup_vg_maxsilu_relu_kernel(tc, tab, y, w, b, offs, out):
                         stop=r == row_blocks - 1,
                     )
 
-        for c in range(pieces):
-            for m in range(out_blocks):
-                result = work.tile([P, PIECE], F32, name="result")
-                nc.scalar.activation(result[:], sums[m][c][:], RELU, bias=bias[:, m : m + 1])
-                nc.sync.dma_start(out[m * P : (m + 1) * P, c * PIECE : (c + 1) * PIECE], result[:])
+                if r == row_blocks - 1:
+                    for m in range(out_blocks):
+                        result = work.tile([P, PIECE], F32, name="result")
+                        if c == pieces - 1 and m == out_blocks - 1:
+                            nc.vector.tensor_scalar(result[:], sums[m][c][:], bias[:, m : m + 1], 0.0, ADD, MAX)
+                        else:
+                            nc.scalar.activation(result[:], sums[m][c][:], RELU, bias=bias[:, m : m + 1])
+                        nc.sync.dma_start(out[m * P : (m + 1) * P, columns], result[:])

@@ -25,53 +25,63 @@ def tile_lookup_vg_maxsilu_relu_kernel(tc, tab, y, w, b, offs, out):
         offsets = held.tile([P, n // 16], U16, name="offsets")
         nc.sync.dma_start(offsets[:], offs)
 
-        values, gates, streams = [], [], []
+        values = [held.tile([P, places], F32, name=f"value{r}") for r in range(row_blocks)]
+        gates = [held.tile([P, places], F32, name=f"gate{r}") for r in range(row_blocks)]
+        streams = [held.tile([P, n], F32, name=f"stream{r}") for r in range(row_blocks)]
+        weights = held.tile([P, row_blocks, width], BF16, name="weights")
+        bias = held.tile([P, out_blocks], F32, name="bias")
+
         half = n // 2
         for r in range(row_blocks):
             block = slice(r * P, (r + 1) * P)
-            value = held.tile([P, places], F32, name=f"value{r}")
-            gate = held.tile([P, places], F32, name=f"gate{r}")
-            stream = held.tile([P, n], F32, name=f"stream{r}")
-            nc.sync.dma_start(value[:], tab[0, block, :])
-            nc.sync.dma_start(stream[:, :half], y[block, :half])
-            nc.sync.dma_start(gate[:], tab[1, block, :])
-            nc.sync.dma_start(stream[:, half:], y[block, half:])
-            values.append(value)
-            gates.append(gate)
-            streams.append(stream)
+            nc.sync.dma_start(values[r][:], tab[0, block, :])
+            nc.sync.dma_start(streams[r][:, :half], y[block, :half])
+            nc.sync.dma_start(gates[r][:], tab[1, block, :])
             if r == 0:
-                weights = held.tile([P, row_blocks, width], BF16, name="weights")
                 nc.sync.dma_start(weights[:], w.rearrange("(k p) m -> p k m", p=P))
-                bias = held.tile([P, out_blocks], F32, name="bias")
-                with nc.allow_non_contiguous_dma(reason="256 single values, one to a partition and block"):
-                    nc.sync.dma_start(bias[:], b.rearrange("(m p) o -> p (m o)", p=P))
+            nc.sync.dma_start(streams[r][:, half:], y[block, half:])
+        with nc.allow_non_contiguous_dma(reason="256 single values, one to a partition and block"):
+            nc.sync.dma_start(bias[:], b.rearrange("(m p) o -> p (m o)", p=P))
 
         sums = [[psum.tile([P, PIECE], F32, name=f"sum{m}_{c}") for c in range(pieces)] for m in range(out_blocks)]
 
-        for r in range(row_blocks):
-            for c in range(pieces):
-                columns = slice(c * PIECE, (c + 1) * PIECE)
-                listed = offsets[:, c * piece_offsets : (c + 1) * piece_offsets]
-                silu = work.tile([P, PIECE], F32, name="silu")
-                nc.scalar.activation(silu[:], gates[r][:].indirect(listed), SILU)
-                top = work.tile([P, PIECE], F32, name="top")
-                nc.vector.tensor_tensor(top[:], values[r][:].indirect(listed), streams[r][:, columns], MAX)
-                x = work.tile([P, PIECE], BF16, name="x")
-                nc.vector.tensor_tensor(x[:], top[:], silu[:], MULT)
-                for m in range(out_blocks):
-                    nc.tensor.matmul(
-                        sums[m][c][:],
-                        weights[:, r, m * P : (m + 1) * P],
-                        x[:],
-                        start=r == 0,
-                        stop=r == row_blocks - 1,
-                    )
+        def look_up(r, c):
+            listed = offsets[:, c * piece_offsets : (c + 1) * piece_offsets]
+            silu = work.tile([P, PIECE], F32, name="silu")
+            nc.scalar.activation(silu[:], gates[r][:].indirect(listed), SILU)
+            top = work.tile([P, PIECE], F32, name="top")
+            nc.vector.tensor_tensor(
+                top[:], values[r][:].indirect(listed), streams[r][:, c * PIECE : (c + 1) * PIECE], MAX
+            )
+            return top, silu
 
-                if r == row_blocks - 1:
-                    for m in range(out_blocks):
-                        result = work.tile([P, PIECE], F32, name="result")
-                        if c == pieces - 1 and m == out_blocks - 1:
-                            nc.vector.tensor_scalar(result[:], sums[m][c][:], bias[:, m : m + 1], 0.0, ADD, MAX)
-                        else:
-                            nc.scalar.activation(result[:], sums[m][c][:], RELU, bias=bias[:, m : m + 1])
-                        nc.sync.dma_start(out[m * P : (m + 1) * P, columns], result[:])
+        def multiply(r, c, top, silu):
+            x = work.tile([P, PIECE], BF16, name="x")
+            nc.vector.tensor_tensor(x[:], top[:], silu[:], MULT)
+            for m in range(out_blocks):
+                nc.tensor.matmul(
+                    sums[m][c][:],
+                    weights[:, r, m * P : (m + 1) * P],
+                    x[:],
+                    start=r == 0,
+                    stop=r == row_blocks - 1,
+                )
+
+        def store(c):
+            for m in range(out_blocks):
+                result = work.tile([P, PIECE], F32, name="result")
+                if c >= pieces - 2 and m % 2 == 1:
+                    nc.vector.tensor_scalar(result[:], sums[m][c][:], bias[:, m : m + 1], 0.0, ADD, MAX)
+                else:
+                    nc.scalar.activation(result[:], sums[m][c][:], RELU, bias=bias[:, m : m + 1])
+                nc.sync.dma_start(out[m * P : (m + 1) * P, c * PIECE : (c + 1) * PIECE], result[:])
+
+        steps = [(r, c) for r in range(row_blocks) for c in range(pieces)]
+        ahead = look_up(*steps[0])
+        for i, (r, c) in enumerate(steps):
+            top, silu = ahead
+            if i + 1 < len(steps):
+                ahead = look_up(*steps[i + 1])
+            multiply(r, c, top, silu)
+        for c in range(pieces):
+            store(c)

@@ -31,15 +31,17 @@ def tile_lookup_vg_maxsilu_relu_kernel(tc, tab, y, w, b, offs, out):
         weights = held.tile([P, row_blocks, width], BF16, name="weights")
         bias = held.tile([P, out_blocks], F32, name="bias")
 
-        half = n // 2
         for r in range(row_blocks):
             block = slice(r * P, (r + 1) * P)
+            early = 2 if r == 0 else 1
             nc.sync.dma_start(values[r][:], tab[0, block, :])
-            nc.sync.dma_start(streams[r][:, :half], y[block, :half])
-            nc.sync.dma_start(gates[r][:], tab[1, block, :])
+            for c in range(pieces):
+                if c == early:
+                    nc.sync.dma_start(gates[r][:], tab[1, block, :])
+                columns = slice(c * PIECE, (c + 1) * PIECE)
+                nc.sync.dma_start(streams[r][:, columns], y[block, columns])
             if r == 0:
                 nc.sync.dma_start(weights[:], w.rearrange("(k p) m -> p k m", p=P))
-            nc.sync.dma_start(streams[r][:, half:], y[block, half:])
         with nc.allow_non_contiguous_dma(reason="256 single values, one to a partition and block"):
             nc.sync.dma_start(bias[:], b.rearrange("(m p) o -> p (m o)", p=P))
 
@@ -83,5 +85,5 @@ def tile_lookup_vg_maxsilu_relu_kernel(tc, tab, y, w, b, offs, out):
             if i + 1 < len(steps):
                 ahead = look_up(*steps[i + 1])
             multiply(r, c, top, silu)
-        for c in range(pieces):
-            store(c)
+            if r == row_blocks - 1:
+                store(c)

import concourse.mybir as mybir

F32, BF16, U16 = mybir.dt.float32, mybir.dt.bfloat16, mybir.dt.uint16
ADD, MAX, MULT = mybir.AluOpType.add, mybir.AluOpType.max, mybir.AluOpType.mult
SILU, RELU = mybir.ActivationFunctionType.Silu, mybir.ActivationFunctionType.Relu

P = 128
PIECE = 512
FLOPS = 2 * 256 * 256 * 2048


def tile_lookup_vg_maxsilu_relu_kernel(tc, tab, y, w, b, offs, out):
    nc = tc.nc
    rows, places = tab.shape[1], tab.shape[2]
    n = y.shape[1]
    width = w.shape[1]
    row_blocks, out_blocks, pieces = rows // P, width // P, n // PIECE
    piece_offsets = PIECE // 16

    with (
        tc.tile_pool(name="held", bufs=1) as held,
        tc.tile_pool(name="work", bufs=row_blocks * pieces) as work,
        tc.psum_pool(name="psum", bufs=1) as psum,
    ):
        offsets = held.tile([P, n // 16], U16, name="offsets")
        nc.sync.dma_start(offsets[:], offs)

        values = [held.tile([P, places], F32, name=f"value{r}") for r in range(row_blocks)]
        gates = [held.tile([P, places], F32, name=f"gate{r}") for r in range(row_blocks)]
        streams = [held.tile([P, n], F32, name=f"stream{r}") for r in range(row_blocks)]
        weights = held.tile([P, row_blocks, width], BF16, name="weights")
        bias = held.tile([P, out_blocks], F32, name="bias")

        for r in range(row_blocks):
            block = slice(r * P, (r + 1) * P)
            early = 2 if r == 0 else 1
            nc.sync.dma_start(values[r][:], tab[0, block, :])
            for c in range(pieces):
                if c == early:
                    nc.sync.dma_start(gates[r][:], tab[1, block, :])
                columns = slice(c * PIECE, (c + 1) * PIECE)
                nc.sync.dma_start(streams[r][:, columns], y[block, columns])
            if r == 0:
                nc.sync.dma_start(weights[:], w.rearrange("(k p) m -> p k m", p=P))
        with nc.allow_non_contiguous_dma(reason="256 single values, one to a partition and block"):
            nc.sync.dma_start(bias[:], b.rearrange("(m p) o -> p (m o)", p=P))

        sums = [[psum.tile([P, PIECE], F32, name=f"sum{m}_{c}") for c in range(pieces)] for m in range(out_blocks)]

        def look_up(r, c):
            listed = offsets[:, c * piece_offsets : (c + 1) * piece_offsets]
            silu = work.tile([P, PIECE], F32, name="silu")
            nc.scalar.activation(silu[:], gates[r][:].indirect(listed), SILU)
            top = work.tile([P, PIECE], F32, name="top")
            nc.vector.tensor_tensor(
                top[:], values[r][:].indirect(listed), streams[r][:, c * PIECE : (c + 1) * PIECE], MAX
            )
            return top, silu

        def multiply(r, c, top, silu):
            x = work.tile([P, PIECE], BF16, name="x")
            nc.vector.tensor_tensor(x[:], top[:], silu[:], MULT)
            for m in range(out_blocks):
                nc.tensor.matmul(
                    sums[m][c][:],
                    weights[:, r, m * P : (m + 1) * P],
                    x[:],
                    start=r == 0,
                    stop=r == row_blocks - 1,
                )

        def store(c):
            for m in range(out_blocks):
                result = work.tile([P, PIECE], F32, name="result")
                if c >= pieces - 2 and m % 2 == 1:
                    nc.vector.tensor_scalar(result[:], sums[m][c][:], bias[:, m : m + 1], 0.0, ADD, MAX)
                else:
                    nc.scalar.activation(result[:], sums[m][c][:], RELU, bias=bias[:, m : m + 1])
                nc.sync.dma_start(out[m * P : (m + 1) * P, c * PIECE : (c + 1) * PIECE], result[:])

        steps = [(r, c) for r in range(row_blocks) for c in range(pieces)]
        ahead = look_up(*steps[0])
        for i, (r, c) in enumerate(steps):
            top, silu = ahead
            if i + 1 < len(steps):
                ahead = look_up(*steps[i + 1])
            multiply(r, c, top, silu)
            if r == row_blocks - 1:
                store(c)
